import numpy as np, ml_dtypes
CORES = [7,135,263,391,15,143,271,399,23,151,279,407,31,159,287,415]
N = 16
def setup_inputs(rng):
    return {"x": rng.standard_normal((N, 128, 128), dtype=np.float32).astype(ml_dtypes.bfloat16)}
def reference(x):
    g = np.concatenate(list(x), axis=1)
    return {"y": np.broadcast_to(g, (N,) + g.shape)}

@@ -1,0 +1,60 @@
+from concourse.bass import DstId, RemoteDMATransfer
+
+SCRATCH = {
+    "img": ("sbuf", [128, 2048], "bfloat16"),
+}
+SEMAPHORES = ["ld", "st", "cab", "mown", "mcab", "plane", "sent"]
+
+CABLED = {0: 3, 3: 0, 1: 2, 2: 1}
+
+
+def rank_program(g, core, T, topo):
+    rank = T.rank_of(core)
+    if rank is None:
+        return
+    h, c = rank % 4, rank // 4
+
+    def rk(hh, cc):
+        return 4 * cc + hh
+
+    def blk(r):
+        return T.img[:, 128 * r:128 * (r + 1)]
+
+    sent = [0]
+
+    def send(r, dst_ranks, sem):
+        ids = []
+        for d in dst_ranks:
+            rid, pid = topo.addr(T.cores[d], core)
+            ids.append(DstId(rid=rid, pnc=pid))
+        g.remote_dma_fused(
+            [RemoteDMATransfer(dst_ids=ids, dma_engine_mask=0xFF, remote_sem=sem, srcs=[blk(r)],
+                               dsts=[blk(r) for _d in dst_ranks], alu_op=0)],
+            local_sem=T.sem.sent)
+        sent[0] += 8
+
+    hc = CABLED[h]
+    hr = h ^ 1
+    cm = c ^ 1
+    peers = [rk(h, c ^ 2), rk(hr, c), rk(hr, c ^ 2)]
+
+    g.dma_start(blk(rank), T.x[:]).then_inc(T.sem.ld, 16)
+    g.wait_ge(T.sem.ld, 16)
+    send(rank, [rk(hc, c)], T.sem.cab)
+    send(rank, [rk(h, cm)], T.sem.mown)
+    send(rank, peers, T.sem.plane)
+
+    g.wait_ge(T.sem.cab, 8)
+    send(rk(hc, c), [rk(h, cm)], T.sem.mcab)
+    send(rk(hc, c), peers, T.sem.plane)
+
+    g.wait_ge(T.sem.mown, 8)
+    send(rk(h, cm), peers, T.sem.plane)
+
+    g.wait_ge(T.sem.mcab, 8)
+    send(rk(hc, cm), peers, T.sem.plane)
+
+    g.wait_ge(T.sem.plane, 96)
+    g.wait_ge(T.sem.sent, sent[0])
+    g.dma_start(T.y[:], T.img[:]).then_inc(T.sem.st, 16)
+    g.wait_ge(T.sem.st, 16)

@@ -1,60 +1,66 @@
 from concourse.bass import DstId, RemoteDMATransfer
 
 SCRATCH = {
-    "img": ("sbuf", [128, 2048], "bfloat16"),
+    "blk": ("dram", [16, 128, 128], "bfloat16"),
 }
-SEMAPHORES = ["ld", "st", "cab", "mown", "mcab", "plane", "sent"]
+SEMAPHORES = ["ld", "st", "sent"] + ["a%d" % j for j in range(16)]
 
 CABLED = {0: 3, 3: 0, 1: 2, 2: 1}
+RANK_CORE, HELPER_CORE = 7, 3
+OFF_CHIP = 0xFF
 
 
 def rank_program(g, core, T, topo):
-    rank = T.rank_of(core)
-    if rank is None:
+    h, c, k = topo.host(core), topo.chip(core), core % 8
+    if c > 3 or k not in (RANK_CORE, HELPER_CORE):
         return
-    h, c = rank % 4, rank // 4
 
     def rk(hh, cc):
         return 4 * cc + hh
 
-    def blk(r):
-        return T.img[:, 128 * r:128 * (r + 1)]
+    def world(hh, cc, kk):
+        return 128 * hh + 8 * cc + kk
 
     sent = [0]
 
-    def send(r, dst_ranks, sem):
+    def send(j, dst_cores):
         ids = []
-        for d in dst_ranks:
-            rid, pid = topo.addr(T.cores[d], core)
+        for d in dst_cores:
+            rid, pid = topo.addr(d, core)
             ids.append(DstId(rid=rid, pnc=pid))
         g.remote_dma_fused(
-            [RemoteDMATransfer(dst_ids=ids, dma_engine_mask=0xFF, remote_sem=sem, srcs=[blk(r)],
-                               dsts=[blk(r) for _d in dst_ranks], alu_op=0)],
+            [RemoteDMATransfer(dst_ids=ids, dma_engine_mask=OFF_CHIP, remote_sem=T.sem["a%d" % j], srcs=[T.blk[j]],
+                               dsts=[T.blk[j] for _d in dst_cores], alu_op=0)],
             local_sem=T.sem.sent)
         sent[0] += 8
 
-    hc = CABLED[h]
-    hr = h ^ 1
-    cm = c ^ 1
-    peers = [rk(h, c ^ 2), rk(hr, c), rk(hr, c ^ 2)]
+    hc, hr, cm = CABLED[h], h ^ 1, c ^ 1
+    plane = [(hr, c), (h, c ^ 2), (hr, c ^ 2)]
+    cross = [(hr, cm), (h, cm ^ 2), (hr, cm ^ 2)]
 
-    g.dma_start(blk(rank), T.x[:]).then_inc(T.sem.ld, 16)
+    if k == HELPER_CORE:
+        kb = rk(hc, c)
+        g.wait_ge(T.sem["a%d" % kb], 8)
+        send(kb, [world(hh, cc, RANK_CORE) for hh, cc in [(h, c), (h, cm)] + plane + cross])
+        g.wait_ge(T.sem.sent, sent[0])
+        return
+
+    me = rk(h, c)
+    g.sync.dma_start(T.blk[me], T.x[:]).then_inc(T.sem.ld, 16)
+    g.scalar.dma_start(T.y[:, 128 * me:128 * (me + 1)], T.x[:]).then_inc(T.sem.st, 16)
+
+    order = ([rk(h, cm)] + [rk(*p) for p in plane] + [rk(*p) for p in cross]
+             + [rk(CABLED[hh], cc) for hh, cc in [(h, c), (h, cm)] + plane + cross])
+    for i, j in enumerate(order):
+        q = g.sync if i % 2 else g.scalar
+        q.wait_ge(T.sem["a%d" % j], 8)
+        q.dma_start(T.y[:, 128 * j:128 * (j + 1)], T.blk[j]).then_inc(T.sem.st, 16)
+
     g.wait_ge(T.sem.ld, 16)
-    send(rank, [rk(hc, c)], T.sem.cab)
-    send(rank, [rk(h, cm)], T.sem.mown)
-    send(rank, peers, T.sem.plane)
-
-    g.wait_ge(T.sem.cab, 8)
-    send(rk(hc, c), [rk(h, cm)], T.sem.mcab)
-    send(rk(hc, c), peers, T.sem.plane)
-
-    g.wait_ge(T.sem.mown, 8)
-    send(rk(h, cm), peers, T.sem.plane)
-
-    g.wait_ge(T.sem.mcab, 8)
-    send(rk(hc, cm), peers, T.sem.plane)
-
-    g.wait_ge(T.sem.plane, 96)
+    send(me, [world(hc, c, HELPER_CORE)])
+    send(me, [world(hh, cc, RANK_CORE) for hh, cc in plane + [(h, cm)]])
+    for p in plane:
+        g.wait_ge(T.sem["a%d" % rk(*p)], 8)
+        send(rk(*p), [world(h, cm, RANK_CORE)])
     g.wait_ge(T.sem.sent, sent[0])
-    g.dma_start(T.y[:], T.img[:]).then_inc(T.sem.st, 16)
-    g.wait_ge(T.sem.st, 16)
+    g.wait_ge(T.sem.st, 16 * 16)

@@ -1,66 +1,87 @@
 from concourse.bass import DstId, RemoteDMATransfer
 
 SCRATCH = {
-    "blk": ("dram", [16, 128, 128], "bfloat16"),
+    "ob": ("dram", [8, 128, 128], "bfloat16"),
+    "kb": ("dram", [9, 4, 128, 32], "bfloat16"),
 }
-SEMAPHORES = ["ld", "st", "sent"] + ["a%d" % j for j in range(16)]
+SEMAPHORES = ["ldo", "ldk", "st", "sent"] + ["a%d" % j for j in range(16)]
 
 CABLED = {0: 3, 3: 0, 1: 2, 2: 1}
-RANK_CORE, HELPER_CORE = 7, 3
-OFF_CHIP = 0xFF
+QUARTERS = {6: [(0, 0xFF)], 2: [(1, 0xFF)], 3: [(2, 0x0F), (3, 0xF0)]}
+CABLE_MASK = [0x03, 0x0C, 0x30, 0xC0]
+K_WHOLE = 24
 
 
 def rank_program(g, core, T, topo):
     h, c, k = topo.host(core), topo.chip(core), core % 8
-    if c > 3 or k not in (RANK_CORE, HELPER_CORE):
+    if c > 3 or k not in (2, 3, 6, 7):
         return
 
     def rk(hh, cc):
         return 4 * cc + hh
 
-    def world(hh, cc, kk):
-        return 128 * hh + 8 * cc + kk
+    def slot(j):
+        return 2 * (j // 4) + (j % 4) % 2
+
+    def sem(j):
+        return T.sem["a%d" % j]
+
+    def ids(places, kk):
+        out = []
+        for hh, cc in places:
+            rid, pid = topo.addr(128 * hh + 8 * cc + kk, core)
+            out.append(DstId(rid=rid, pnc=pid))
+        return out
 
     sent = [0]
 
-    def send(j, dst_cores):
-        ids = []
-        for d in dst_cores:
-            rid, pid = topo.addr(d, core)
-            ids.append(DstId(rid=rid, pnc=pid))
-        g.remote_dma_fused(
-            [RemoteDMATransfer(dst_ids=ids, dma_engine_mask=OFF_CHIP, remote_sem=T.sem["a%d" % j], srcs=[T.blk[j]],
-                               dsts=[T.blk[j] for _d in dst_cores], alu_op=0)],
-            local_sem=T.sem.sent)
-        sent[0] += 8
+    def fused(transfers, engines):
+        g.remote_dma_fused(transfers, local_sem=T.sem.sent)
+        sent[0] += engines
+
+    def send_o(j, dst_ids):
+        o = T.ob[slot(j)]
+        fused([RemoteDMATransfer(dst_ids=dst_ids, dma_engine_mask=0xFF, remote_sem=sem(j), srcs=[o],
+                                 dsts=[o for _d in dst_ids], alu_op=0)], 8)
 
     hc, hr, cm = CABLED[h], h ^ 1, c ^ 1
     plane = [(hr, c), (h, c ^ 2), (hr, c ^ 2)]
     cross = [(hr, cm), (h, cm ^ 2), (hr, cm ^ 2)]
+    fan = [(h, c), (h, cm)] + plane + cross
 
-    if k == HELPER_CORE:
-        kb = rk(hc, c)
-        g.wait_ge(T.sem["a%d" % kb], 8)
-        send(kb, [world(hh, cc, RANK_CORE) for hh, cc in [(h, c), (h, cm)] + plane + cross])
+    if k != 7:
+        kj = rk(hc, c)
+        mine = QUARTERS[k]
+        g.wait_ge(sem(kj), 2 * len(mine))
+        dst = ids(fan, 7)
+        fused([RemoteDMATransfer(dst_ids=dst, dma_engine_mask=m, remote_sem=sem(kj), srcs=[T.kb[slot(kj), q]],
+                                 dsts=[T.kb[slot(kj), q] for _d in dst], alu_op=0) for q, m in mine], 8)
+        if k == 2:
+            pj = rk(*plane[2])
+            g.wait_ge(sem(pj), 8)
+            send_o(pj, ids([(h, cm), (h, c)], 7))
         g.wait_ge(T.sem.sent, sent[0])
         return
 
     me = rk(h, c)
-    g.sync.dma_start(T.blk[me], T.x[:]).then_inc(T.sem.ld, 16)
-    g.scalar.dma_start(T.y[:, 128 * me:128 * (me + 1)], T.x[:]).then_inc(T.sem.st, 16)
+    g.sync.dma_start(T.kb[8], T.x[:]).then_inc(T.sem.ldk, 16)
+    g.scalar.dma_start(T.ob[slot(me)], T.x[:]).then_inc(T.sem.ldo, 16)
+    g.sync.dma_start(T.y[:, 128 * me:128 * (me + 1)], T.x[:]).then_inc(T.sem.st, 16)
 
-    order = ([rk(h, cm)] + [rk(*p) for p in plane] + [rk(*p) for p in cross]
-             + [rk(CABLED[hh], cc) for hh, cc in [(h, c), (h, cm)] + plane + cross])
-    for i, j in enumerate(order):
+    stores = [(rk(*p), T.ob, 8) for p in [(h, cm)] + plane + cross] + [(rk(CABLED[hh], cc), T.kb, K_WHOLE) for hh, cc in fan]
+    for i, (j, buf, n) in enumerate(stores):
         q = g.sync if i % 2 else g.scalar
-        q.wait_ge(T.sem["a%d" % j], 8)
-        q.dma_start(T.y[:, 128 * j:128 * (j + 1)], T.blk[j]).then_inc(T.sem.st, 16)
+        q.wait_ge(sem(j), n)
+        q.dma_start(T.y[:, 128 * j:128 * (j + 1)], buf[slot(j)]).then_inc(T.sem.st, 16)
 
-    g.wait_ge(T.sem.ld, 16)
-    send(me, [world(hc, c, HELPER_CORE)])
-    send(me, [world(hh, cc, RANK_CORE) for hh, cc in plane + [(h, cm)]])
-    for p in plane:
-        g.wait_ge(T.sem["a%d" % rk(*p)], 8)
-        send(rk(*p), [world(h, cm, RANK_CORE)])
+    g.wait_ge(T.sem.ldk, 16)
+    fused([RemoteDMATransfer(dst_ids=ids([(hc, c)], kk), dma_engine_mask=CABLE_MASK[q], remote_sem=sem(me), srcs=[T.kb[8, q]],
+                             dsts=[T.kb[slot(me), q]], alu_op=0)
+           for kk in (6, 2, 3) for q, _m in QUARTERS[kk]], 8)
+    g.wait_ge(T.sem.ldo, 16)
+    send_o(me, ids(plane[:2], 7) + ids(plane[2:], 2) + ids([(h, cm)], 7))
+    for p in plane[:2]:
+        g.wait_ge(sem(rk(*p)), 8)
+        send_o(rk(*p), ids([(h, cm)], 7))
     g.wait_ge(T.sem.sent, sent[0])
     g.wait_ge(T.sem.st, 16 * 16)

from concourse.bass import DstId, RemoteDMATransfer

SCRATCH = {
    "ob": ("dram", [8, 128, 128], "bfloat16"),
    "kb": ("dram", [9, 4, 128, 32], "bfloat16"),
}
SEMAPHORES = ["ldo", "ldk", "st", "sent"] + ["a%d" % j for j in range(16)]

CABLED = {0: 3, 3: 0, 1: 2, 2: 1}
QUARTERS = {6: [(0, 0xFF)], 2: [(1, 0xFF)], 3: [(2, 0x0F), (3, 0xF0)]}
CABLE_MASK = [0x03, 0x0C, 0x30, 0xC0]
K_WHOLE = 24


def rank_program(g, core, T, topo):
    h, c, k = topo.host(core), topo.chip(core), core % 8
    if c > 3 or k not in (2, 3, 6, 7):
        return

    def rk(hh, cc):
        return 4 * cc + hh

    def slot(j):
        return 2 * (j // 4) + (j % 4) % 2

    def sem(j):
        return T.sem["a%d" % j]

    def ids(places, kk):
        out = []
        for hh, cc in places:
            rid, pid = topo.addr(128 * hh + 8 * cc + kk, core)
            out.append(DstId(rid=rid, pnc=pid))
        return out

    sent = [0]

    def fused(transfers, engines):
        g.remote_dma_fused(transfers, local_sem=T.sem.sent)
        sent[0] += engines

    def send_o(j, dst_ids):
        o = T.ob[slot(j)]
        fused([RemoteDMATransfer(dst_ids=dst_ids, dma_engine_mask=0xFF, remote_sem=sem(j), srcs=[o],
                                 dsts=[o for _d in dst_ids], alu_op=0)], 8)

    hc, hr, cm = CABLED[h], h ^ 1, c ^ 1
    plane = [(hr, c), (h, c ^ 2), (hr, c ^ 2)]
    cross = [(hr, cm), (h, cm ^ 2), (hr, cm ^ 2)]
    fan = [(h, c), (h, cm)] + plane + cross

    if k != 7:
        kj = rk(hc, c)
        mine = QUARTERS[k]
        g.wait_ge(sem(kj), 2 * len(mine))
        dst = ids(fan, 7)
        fused([RemoteDMATransfer(dst_ids=dst, dma_engine_mask=m, remote_sem=sem(kj), srcs=[T.kb[slot(kj), q]],
                                 dsts=[T.kb[slot(kj), q] for _d in dst], alu_op=0) for q, m in mine], 8)
        if k == 2:
            pj = rk(*plane[2])
            g.wait_ge(sem(pj), 8)
            send_o(pj, ids([(h, cm), (h, c)], 7))
        g.wait_ge(T.sem.sent, sent[0])
        return

    me = rk(h, c)
    g.sync.dma_start(T.kb[8], T.x[:]).then_inc(T.sem.ldk, 16)
    g.scalar.dma_start(T.ob[slot(me)], T.x[:]).then_inc(T.sem.ldo, 16)
    g.sync.dma_start(T.y[:, 128 * me:128 * (me + 1)], T.x[:]).then_inc(T.sem.st, 16)

    stores = [(rk(*p), T.ob, 8) for p in [(h, cm)] + plane + cross] + [(rk(CABLED[hh], cc), T.kb, K_WHOLE) for hh, cc in fan]
    for i, (j, buf, n) in enumerate(stores):
        q = g.sync if i % 2 else g.scalar
        q.wait_ge(sem(j), n)
        q.dma_start(T.y[:, 128 * j:128 * (j + 1)], buf[slot(j)]).then_inc(T.sem.st, 16)

    g.wait_ge(T.sem.ldk, 16)
    fused([RemoteDMATransfer(dst_ids=ids([(hc, c)], kk), dma_engine_mask=CABLE_MASK[q], remote_sem=sem(me), srcs=[T.kb[8, q]],
                             dsts=[T.kb[slot(me), q]], alu_op=0)
           for kk in (6, 2, 3) for q, _m in QUARTERS[kk]], 8)
    g.wait_ge(T.sem.ldo, 16)
    send_o(me, ids(plane[:2], 7) + ids(plane[2:], 2) + ids([(h, cm)], 7))
    for p in plane[:2]:
        g.wait_ge(sem(rk(*p)), 8)
        send_o(rk(*p), ids([(h, cm)], 7))
    g.wait_ge(T.sem.sent, sent[0])
    g.wait_ge(T.sem.st, 16 * 16)
